import numpy as np
import ml_dtypes


def mxq(x, axis, fmt="e4m3"):
    dtype, down = {"e4m3": (ml_dtypes.float8_e4m3fn, 7), "e5m2": (ml_dtypes.float8_e5m2, 14)}[fmt]
    v = np.moveaxis(np.asarray(x, np.float32).astype(ml_dtypes.bfloat16).astype(np.float64), axis, -1)
    blocks = v.reshape(v.shape[:-1] + (-1, 32))
    amax = np.abs(blocks).max(-1, keepdims=True)
    byte = np.maximum(np.where(amax > 0, np.frexp(amax)[1] - 1 + 127, 0) - down, 1)
    scale = np.exp2(byte - 127.0)
    codes = (blocks / scale).astype(np.float32).astype(dtype).astype(np.float64)
    return np.moveaxis((codes * scale).reshape(v.shape), -1, axis)


WIDE = False


def mx_kscale(k):
    if not WIDE:
        return np.ones(k)
    levels = np.array([10, -10, 5, -5, 0])
    if k % 512:
        return np.exp2(np.random.permutation(np.resize(levels, k // 32))).repeat(32)
    a = np.empty((k // 512, 16))
    for p in range(k // 512):
        a[p, :8] = np.random.permutation(np.resize(levels, 8))
        for g in range(8):
            far = levels[np.abs(levels - a[p, g]) >= 10]
            a[p, g + 8] = far[np.random.randint(len(far))]
    return np.exp2(a.ravel()).repeat(32)


def f64(x):
    return np.asarray(x).astype(np.float64)


def striped(idx):
    return np.tile(idx.reshape(-1, 16).T, (8, 1)).astype(np.uint16)


def unstriped(offs):
    return offs[:16].T.reshape(-1).astype(np.int64)


def striped8(idx):
    return np.concatenate([x.reshape(-1, 16).T for x in idx]).astype(np.uint16)


def runs(offs, k):
    lists = np.stack([offs[16 * r : 16 * r + 16].T.reshape(-1) for r in range(8)]).astype(np.int64)
    return lists[np.arange(k) % 512 // 64]


def pack_weight(w):
    k, n = w.shape
    w = f64(np.asarray(w, np.float32).astype(ml_dtypes.bfloat16)).reshape(k // 32, 32, n)
    amax = np.abs(w).max(1)
    byte = np.clip(np.where(amax > 0, np.frexp(amax)[1] - 1 + 127 - 7, 1), 1, 254)
    scaled = (w * np.exp2(127.0 - byte)[:, None, :]).reshape(k, n).astype(np.float32)
    words = np.ascontiguousarray(scaled.reshape(k // 512, 128, 4, n).transpose(0, 1, 3, 2)).astype(ml_dtypes.float8_e4m3fn).view(np.uint8)
    return words, np.ascontiguousarray(byte.astype(np.uint8).reshape(k // 512, 16, n))


def unpack_weight(words, scales):
    g, p, n, _ = words.shape
    vals = np.ascontiguousarray(words).view(ml_dtypes.float8_e4m3fn).astype(np.float64) * np.repeat(np.exp2(scales.astype(np.float64) - 127.0), 8, axis=1)[..., None]
    return vals.transpose(0, 1, 3, 2).reshape(g * 512, n)


K, T, S, G, H, C, U = 512, 1024, 512, 2048, 512, 512, 1024


def setup_inputs():
    n = np.random.standard_normal
    s = mx_kscale(K)[:, None]
    packed_xT = pack_weight(n((K, T)) * s)
    packed_dT = pack_weight(n((K, G)) / s)
    return {
        "x_words": packed_xT[0],
        "x_scales": packed_xT[1],
        "d_words": packed_dT[0],
        "d_scales": packed_dT[1],
        "gs": (np.random.uniform(0.5, 1.5, (K, 1)) / s).astype(np.float32),
        "mem": n((C, U)).astype(np.float32),
        "offs": striped(np.random.permutation(T)[:S]),
        "k1": striped8(np.random.randint(0, G, (8, H))),
        "n1": striped8(np.stack([np.random.permutation(S) for _ in range(8)])),
        "n2": striped8(np.stack([np.random.permutation(S) for _ in range(8)])),
        "cand": striped(np.random.permutation(T)[:C]),
        "n3": striped8(np.stack([np.random.permutation(U)[:S] for _ in range(8)])),
    }


def reference(x_words, x_scales, d_words, d_scales, gs, mem, offs, k1, n1, n2, cand, n3):
    x_cand = unpack_weight(x_words, x_scales)[:, unstriped(cand)]
    d_k1 = unpack_weight(d_words, d_scales)[np.arange(K)[:, None], runs(k1, K)]
    xq = unpack_weight(x_words, x_scales)[:, unstriped(offs)]
    h = 0.0625 * (d_k1.T @ xq)
    st = h - (h[np.arange(H)[:, None], runs(n1, H)])
    z = f64(gs) * (np.maximum(st, st[np.arange(H)[:, None], runs(n2, H)]))
    s = 0.0625 * ((x_cand.T @ mxq(z, 0, "e4m3")))
    nw = np.maximum(s, 0.5 * (f64(mem)[np.arange(C)[:, None], runs(n3, C)]))
    out = f64(mem).copy()
    out[np.arange(C)[:, None], runs(n3, C)] = nw
    return out

@@ -1,0 +1,177 @@
+from contextlib import ExitStack
+
+import concourse.mybir as mybir
+
+K, T, S, G, H, C, U = 512, 1024, 512, 2048, 512, 512, 1024
+FLOPS = 2 * K * H * S + 2 * K * C * S
+
+F32 = mybir.dt.float32
+BF16 = mybir.dt.bfloat16
+I32 = mybir.dt.int32
+U32 = mybir.dt.uint32
+U16 = mybir.dt.uint16
+U8 = mybir.dt.uint8
+FP8X4 = mybir.dt.float8_e4m3fn_x4
+ALU = mybir.AluOpType
+COPY = mybir.ActivationFunctionType.Copy
+
+P = 128
+PACK = 4
+HALF = S // 2
+
+
+def tile_picked_pqchopmxpagex_none_p_kernel(
+    tc, x_words, x_scales, d_words, d_scales, gs, mem, offs, k1, n1, n2, cand, n3, out
+):
+    nc = tc.nc
+    with ExitStack() as ctx:
+        keep = ctx.enter_context(tc.tile_pool(name="keep", bufs=1))
+        psum = ctx.enter_context(tc.psum_pool(name="psum", bufs=1))
+
+        def load_list(src, name):
+            t = keep.tile([P, S // 16], U16, name=name)
+            nc.sync.dma_start(t[:], src)
+            return t
+
+        def halves(lst, h):
+            return lst[:, h * (HALF // 16) : (h + 1) * (HALF // 16)]
+
+        def deal(dst, src):
+            nc.vector.tensor_copy(
+                dst.rearrange("p (t m) -> p m t", t=PACK), src.rearrange("p (m t) -> p m t", t=PACK)
+            )
+
+        d_byte_table = keep.tile([P, G], U8, align_bytes=64)
+        x_byte_table = keep.tile([P, T], U8, align_bytes=64)
+        planes = keep.tile([P, 2 * S], U8, align_bytes=64)
+        c_scale = keep.tile([P, C], U8, align_bytes=64)
+        nc.vector.memset(c_scale[:].bitcast(I32), 0)
+        nc.vector.memset(planes[:].bitcast(I32), 0)
+
+        k1_list = load_list(k1, "k1_list")
+        nc.scalar.dma_start(d_byte_table[:].bitcast(I32), d_scales[0].bitcast(I32).unsqueeze(1).to_broadcast([16, 8, G // 4]))
+        offs_list = load_list(offs, "offs_list")
+        nc.scalar.dma_start(x_byte_table[:].bitcast(I32), x_scales[0].bitcast(I32).unsqueeze(1).to_broadcast([16, 8, T // 4]))
+        cand_list = load_list(cand, "cand_list")
+        d_word_table = keep.tile([P, G], I32, align_bytes=64, tag="slot0")
+        nc.sync.dma_start(d_word_table[:], d_words[0].rearrange("p n t -> p (n t)").bitcast(I32))
+        x_word_table = keep.tile([P, T], I32, align_bytes=64, tag="slot1")
+        nc.sync.dma_start(x_word_table[:], x_words[0].rearrange("p n t -> p (n t)").bitcast(I32))
+        n1_list = load_list(n1, "n1_list")
+        n2_list = load_list(n2, "n2_list")
+        n3_list = load_list(n3, "n3_list")
+        gs_sb = keep.tile([P, PACK], F32)
+        nc.sync.dma_start(gs_sb[:], gs.rearrange("(p t) o -> p (t o)", t=PACK))
+
+        def place(plane, staged, queues):
+            src = staged.bitcast(I32)
+            dst = plane.bitcast(I32)
+            for a in range(4):
+                queues[a % 2].dma_start(dst[a:P:32, :], src[8 * a : P : 32, :])
+
+        picked_bytes = keep.tile([P, 2 * S], U8, align_bytes=64)
+        staged = keep.tile([P, 2 * S], U8, align_bytes=64, tag="slot2")
+        nc.vector.tensor_copy(picked_bytes[:, :S], d_byte_table[:].indirect(k1_list[:]))
+        nc.vector.tensor_copy(picked_bytes[:, S:], x_byte_table[:].indirect(offs_list[:]))
+        deal(staged[:, :S], picked_bytes[:, :S])
+        nc.vector.tensor_copy(staged[:, S:].bitcast(I32), picked_bytes[:, S:].bitcast(I32))
+        place(planes[:], staged[:], (nc.sync, nc.scalar))
+        d_scale, xq_scale = planes[:, :S], planes[:, S:]
+
+        d_picked = keep.tile([P, H], U32, align_bytes=64, tag="slot3")
+        nc.vector.tensor_copy(d_picked[:], d_word_table[:].bitcast(U32).indirect(k1_list[:]))
+        xq_codes = keep.tile([P, S], U32, align_bytes=64)
+        nc.vector.tensor_copy(xq_codes[:], x_word_table[:].bitcast(U32).indirect(offs_list[:]))
+        d_codes = keep.tile([P, H], U32, align_bytes=64)
+        deal(d_codes[:], d_picked[:])
+
+        h_neg, h_pos = [], []
+        for t in range(PACK):
+            cols = slice(t * P, (t + 1) * P)
+            acc = psum.tile([P, S], F32, name=f"h_acc{t}")
+            nc.tensor.matmul_mx(
+                out=acc[:], lhsT=d_codes[:, cols].bitcast(FP8X4), lhsT_scale=d_scale[:, cols],
+                rhs=xq_codes[:].bitcast(FP8X4), rhs_scale=xq_scale, start=True, stop=True,
+            )
+            hn = keep.tile([P, S], F32, name=f"h_neg{t}")
+            nc.scalar.activation(hn[:], acc[:], COPY, scale=-0.0625)
+            hp = []
+            for h in range(2):
+                hp.append(keep.tile([P, HALF], F32, name=f"h_pos{t}_{h}", tag=f"h_pos{t}_{h}"))
+                nc.scalar.activation(hp[h][:], acc[:, h * HALF : (h + 1) * HALF], COPY, scale=0.0625)
+            h_neg.append(hn)
+            h_pos.append(hp)
+
+        c_bytes = keep.tile([P, C], U8, align_bytes=64)
+        nc.vector.tensor_copy(c_bytes[:], x_byte_table[:].indirect(cand_list[:]))
+        c_picked = keep.tile([P, C], U32, align_bytes=64)
+        nc.vector.tensor_copy(c_picked[:], x_word_table[:].bitcast(U32).indirect(cand_list[:]))
+        c_staged = keep.tile([P, C], U8, align_bytes=64)
+        deal(c_staged[:], c_bytes[:])
+        place(c_scale[:], c_staged[:], (nc.sync, nc.sync))
+        c_codes = keep.tile([P, C], U32, align_bytes=64)
+        deal(c_codes[:], c_picked[:])
+
+        mem_rows = mem.rearrange("(p t) u -> t p u", t=PACK)
+        out_rows = out.rearrange("(p t) u -> t p u", t=PACK)
+        page = []
+        for t in range(PACK):
+            pg = keep.tile([P, U], F32, name=f"page{t}", tag=f"slot{t}", align_bytes=64)
+            nc.sync.dma_start(pg[:], mem_rows[t])
+            page.append(pg)
+
+        z_bf = keep.tile([P, S, PACK], BF16, align_bytes=64, tag="z_bf")
+        st, other, old = {}, {}, {}
+
+        def subtract(t):
+            st[t] = keep.tile([P, S], F32, name=f"st{t}", tag=f"st{t}")
+            for h in range(2):
+                cols = slice(h * HALF, (h + 1) * HALF)
+                nc.vector.tensor_tensor(st[t][:, cols], h_neg[t][:].indirect(halves(n1_list, h)), h_pos[t][h][:], ALU.add)
+
+        def fetch(t):
+            other[t] = keep.tile([P, S], F32, name=f"other{t}", tag=f"h_pos{t + 1}_0")
+            for h in range(2):
+                cols = slice(h * HALF, (h + 1) * HALF)
+                nc.vector.tensor_copy(other[t][:, cols], st[t][:].indirect(halves(n2_list, h)))
+
+        def larger(t):
+            big = keep.tile([P, S], F32, name=f"big{t}", tag=f"h_pos{t + 2}_1")
+            nc.vector.tensor_tensor(big[:], st[t][:], other[t][:], ALU.max)
+            nc.scalar.activation(z_bf[:, :, t], big[:], COPY, scale=gs_sb[:, t : t + 1])
+
+        def fetch_old(t, tag, align):
+            old[t] = keep.tile([P, S], F32, name=f"old{t}", tag=tag, align_bytes=align)
+            nc.vector.tensor_scalar(old[t][:], page[t][:].indirect(n3_list[:]), 0.5, 0.0, ALU.mult, ALU.add)
+
+        for step in range(PACK + 2):
+            if step < PACK:
+                subtract(step)
+            if 1 <= step <= PACK:
+                fetch(step - 1)
+            if step == PACK + 1:
+                fetch_old(0, "st1", None)
+            if step >= 2:
+                larger(step - 2)
+        fetch_old(1, "st2", None)
+        fetch_old(2, "h_pos3_0", None)
+
+        z_codes = keep.tile([P, S], U32, align_bytes=64)
+        z_scale = keep.tile([P, S], U8, align_bytes=64)
+        nc.vector.quantize_mx(z_codes[:].bitcast(FP8X4), z_scale[:], z_bf[:].rearrange("p s t -> p (s t)"))
+        fetch_old(3, "z_bf", 64)
+
+        nw = {}
+        for t in range(PACK + 1):
+            if t < PACK:
+                cols = slice(t * P, (t + 1) * P)
+                acc = psum.tile([P, S], F32, name=f"s_acc{t}")
+                nc.tensor.matmul_mx(
+                    out=acc[:], lhsT=c_codes[:, cols].bitcast(FP8X4), lhsT_scale=c_scale[:, cols],
+                    rhs=z_codes[:].bitcast(FP8X4), rhs_scale=z_scale[:], start=True, stop=True,
+                )
+                nw[t] = keep.tile([P, S], F32, name=f"nw{t}")
+                nc.vector.scalar_tensor_tensor(nw[t][:], acc[:], 0.0625, old[t][:], ALU.mult, ALU.max)
+            if t >= 1:
+                nc.vector.tensor_copy(page[t - 1][:].indirect(n3_list[:]), nw[t - 1][:])
+                nc.sync.dma_start(out_rows[t - 1], page[t - 1][:])

@@ -14,6 +14,7 @@ U8 = mybir.dt.uint8
 FP8X4 = mybir.dt.float8_e4m3fn_x4
 ALU = mybir.AluOpType
 COPY = mybir.ActivationFunctionType.Copy
+RELU = mybir.ActivationFunctionType.Relu
 
 P = 128
 PACK = 4
@@ -36,9 +37,10 @@ def tile_picked_pqchopmxpagex_none_p_kernel(
         def halves(lst, h):
             return lst[:, h * (HALF // 16) : (h + 1) * (HALF // 16)]
 
-        def deal(dst, src):
+        def deal(dst, src, run):
             nc.vector.tensor_copy(
-                dst.rearrange("p (t m) -> p m t", t=PACK), src.rearrange("p (m t) -> p m t", t=PACK)
+                dst.rearrange("p (t c i) -> p c t i", t=PACK, i=run),
+                src.rearrange("p (c i t) -> p c t i", t=PACK, i=run),
             )
 
         d_byte_table = keep.tile([P, G], U8, align_bytes=64)
@@ -48,20 +50,23 @@ def tile_picked_pqchopmxpagex_none_p_kernel(
         nc.vector.memset(c_scale[:].bitcast(I32), 0)
         nc.vector.memset(planes[:].bitcast(I32), 0)
 
-        k1_list = load_list(k1, "k1_list")
-        nc.scalar.dma_start(d_byte_table[:].bitcast(I32), d_scales[0].bitcast(I32).unsqueeze(1).to_broadcast([16, 8, G // 4]))
         offs_list = load_list(offs, "offs_list")
-        nc.scalar.dma_start(x_byte_table[:].bitcast(I32), x_scales[0].bitcast(I32).unsqueeze(1).to_broadcast([16, 8, T // 4]))
-        cand_list = load_list(cand, "cand_list")
+        nc.sync.dma_start(x_byte_table[:].bitcast(I32), x_scales[0].bitcast(I32).unsqueeze(1).to_broadcast([16, 8, T // 4]))
+        k1_list = load_list(k1, "k1_list")
+        nc.sync.dma_start(d_byte_table[:].bitcast(I32), d_scales[0].bitcast(I32).unsqueeze(1).to_broadcast([16, 8, G // 4]))
+        n2_list = load_list(n2, "n2_list")
         d_word_table = keep.tile([P, G], I32, align_bytes=64, tag="slot0")
         nc.sync.dma_start(d_word_table[:], d_words[0].rearrange("p n t -> p (n t)").bitcast(I32))
         x_word_table = keep.tile([P, T], I32, align_bytes=64, tag="slot1")
         nc.sync.dma_start(x_word_table[:], x_words[0].rearrange("p n t -> p (n t)").bitcast(I32))
-        n1_list = load_list(n1, "n1_list")
-        n2_list = load_list(n2, "n2_list")
         n3_list = load_list(n3, "n3_list")
-        gs_sb = keep.tile([P, PACK], F32)
-        nc.sync.dma_start(gs_sb[:], gs.rearrange("(p t) o -> p (t o)", t=PACK))
+        cand_list = load_list(cand, "cand_list")
+        n1_list = load_list(n1, "n1_list")
+        h_sb = [keep.tile([P, 2 * S], F32, name=f"h{t}") for t in range(PACK)]
+        st = [keep.tile([P, 2 * S], F32, name=f"st{t}", tag=f"st{t}") for t in range(PACK)]
+        for t in range(PACK):
+            nc.vector.memset(h_sb[t][:, S:], 0.0)
+            nc.gpsimd.memset(st[t][:, S:], 0.0)
 
         def place(plane, staged, queues):
             src = staged.bitcast(I32)
@@ -69,93 +74,93 @@ def tile_picked_pqchopmxpagex_none_p_kernel(
             for a in range(4):
                 queues[a % 2].dma_start(dst[a:P:32, :], src[8 * a : P : 32, :])
 
-        picked_bytes = keep.tile([P, 2 * S], U8, align_bytes=64)
+        xq_bytes = keep.tile([P, S], U8, align_bytes=64, tag="slot5")
+        d_bytes = keep.tile([P, H], U8, align_bytes=64)
         staged = keep.tile([P, 2 * S], U8, align_bytes=64, tag="slot2")
-        nc.vector.tensor_copy(picked_bytes[:, :S], d_byte_table[:].indirect(k1_list[:]))
-        nc.vector.tensor_copy(picked_bytes[:, S:], x_byte_table[:].indirect(offs_list[:]))
-        deal(staged[:, :S], picked_bytes[:, :S])
-        nc.vector.tensor_copy(staged[:, S:].bitcast(I32), picked_bytes[:, S:].bitcast(I32))
+        nc.vector.tensor_copy(xq_bytes[:], x_byte_table[:].indirect(offs_list[:]))
+        nc.vector.tensor_copy(d_bytes[:], d_byte_table[:].indirect(k1_list[:]))
+        nc.vector.tensor_copy(staged[:, S:].bitcast(I32), xq_bytes[:].bitcast(I32))
+        deal(staged[:, :S], d_bytes[:], 16)
         place(planes[:], staged[:], (nc.sync, nc.scalar))
         d_scale, xq_scale = planes[:, :S], planes[:, S:]
 
+        gs_sb = keep.tile([P, PACK], F32, align_bytes=64, tag="slot5")
+        nc.sync.dma_start(gs_sb[:], gs.rearrange("(p t) o -> p (t o)", t=PACK))
         d_picked = keep.tile([P, H], U32, align_bytes=64, tag="slot3")
         nc.vector.tensor_copy(d_picked[:], d_word_table[:].bitcast(U32).indirect(k1_list[:]))
         xq_codes = keep.tile([P, S], U32, align_bytes=64)
         nc.vector.tensor_copy(xq_codes[:], x_word_table[:].bitcast(U32).indirect(offs_list[:]))
         d_codes = keep.tile([P, H], U32, align_bytes=64)
-        deal(d_codes[:], d_picked[:])
+        deal(d_codes[:].bitcast(I32), d_picked[:].bitcast(I32), 4)
 
-        h_neg, h_pos = [], []
         for t in range(PACK):
             cols = slice(t * P, (t + 1) * P)
-            acc = psum.tile([P, S], F32, name=f"h_acc{t}")
+            acc = psum.tile([P, S], F32, name=f"h_acc{t}", tag=f"bank{PACK + t}")
             nc.tensor.matmul_mx(
                 out=acc[:], lhsT=d_codes[:, cols].bitcast(FP8X4), lhsT_scale=d_scale[:, cols],
                 rhs=xq_codes[:].bitcast(FP8X4), rhs_scale=xq_scale, start=True, stop=True,
             )
-            hn = keep.tile([P, S], F32, name=f"h_neg{t}")
-            nc.scalar.activation(hn[:], acc[:], COPY, scale=-0.0625)
-            hp = []
-            for h in range(2):
-                hp.append(keep.tile([P, HALF], F32, name=f"h_pos{t}_{h}", tag=f"h_pos{t}_{h}"))
-                nc.scalar.activation(hp[h][:], acc[:, h * HALF : (h + 1) * HALF], COPY, scale=0.0625)
-            h_neg.append(hn)
-            h_pos.append(hp)
+            nc.scalar.activation(h_sb[t][:, :S], acc[:], COPY, scale=0.0625)
 
-        c_bytes = keep.tile([P, C], U8, align_bytes=64)
+        c_bytes = keep.tile([P, C], U8, align_bytes=64, tag="slot3")
         nc.vector.tensor_copy(c_bytes[:], x_byte_table[:].indirect(cand_list[:]))
-        c_picked = keep.tile([P, C], U32, align_bytes=64)
-        nc.vector.tensor_copy(c_picked[:], x_word_table[:].bitcast(U32).indirect(cand_list[:]))
-        c_staged = keep.tile([P, C], U8, align_bytes=64)
-        deal(c_staged[:], c_bytes[:])
-        place(c_scale[:], c_staged[:], (nc.sync, nc.sync))
         c_codes = keep.tile([P, C], U32, align_bytes=64)
-        deal(c_codes[:], c_picked[:])
+        nc.vector.tensor_copy(
+            c_codes[:].rearrange("p (t g v) -> p g t v", t=PACK, v=8), x_word_table[:].bitcast(U32).indirect(cand_list[:])
+        )
+        c_staged = keep.tile([P, C], U8, align_bytes=64, tag="slot4")
+        nc.vector.tensor_copy(
+            c_staged[:].bitcast(I32).rearrange("p (t g w) -> p g t w", t=PACK, w=2),
+            c_bytes[:].bitcast(I32).rearrange("p (g t w) -> p g t w", t=PACK, w=2),
+        )
+        place(c_scale[:], c_staged[:], (nc.sync, nc.sync))
 
-        mem_rows = mem.rearrange("(p t) u -> t p u", t=PACK)
-        out_rows = out.rearrange("(p t) u -> t p u", t=PACK)
+        mem_rows = mem.rearrange("(g t v) u -> t g v u", t=PACK, v=8)
+        out_rows = out.rearrange("(g t v) u -> t g v u", t=PACK, v=8)
         page = []
         for t in range(PACK):
-            pg = keep.tile([P, U], F32, name=f"page{t}", tag=f"slot{t}", align_bytes=64)
+            pg = keep.tile([P, U], F32, name=f"page{t}", tag=f"slot{(0, 1, 2, 4)[t]}", align_bytes=64)
             nc.sync.dma_start(pg[:], mem_rows[t])
             page.append(pg)
 
+        z_pairs = keep.tile([P, 2, S, 2], BF16, align_bytes=64)
         z_bf = keep.tile([P, S, PACK], BF16, align_bytes=64, tag="z_bf")
-        st, other, old = {}, {}, {}
+        other, old = {}, {}
 
         def subtract(t):
-            st[t] = keep.tile([P, S], F32, name=f"st{t}", tag=f"st{t}")
-            for h in range(2):
-                cols = slice(h * HALF, (h + 1) * HALF)
-                nc.vector.tensor_tensor(st[t][:, cols], h_neg[t][:].indirect(halves(n1_list, h)), h_pos[t][h][:], ALU.add)
+            far = keep.tile([P, S], F32, name=f"far{t}", tag=f"far{t}")
+            nc.vector.tensor_copy(far[:], h_sb[t][:].indirect(n1_list[:]))
+            nc.gpsimd.tensor_tensor(st[t][:, :S], h_sb[t][:, :S], far[:], ALU.subtract)
 
         def fetch(t):
-            other[t] = keep.tile([P, S], F32, name=f"other{t}", tag=f"h_pos{t + 1}_0")
-            for h in range(2):
-                cols = slice(h * HALF, (h + 1) * HALF)
-                nc.vector.tensor_copy(other[t][:, cols], st[t][:].indirect(halves(n2_list, h)))
+            other[t] = keep.tile([P, S], F32, name=f"other{t}", tag=f"other{t}")
+            nc.vector.tensor_copy(other[t][:], st[t][:].indirect(n2_list[:]))
 
         def larger(t):
-            big = keep.tile([P, S], F32, name=f"big{t}", tag=f"h_pos{t + 2}_1")
-            nc.vector.tensor_tensor(big[:], st[t][:], other[t][:], ALU.max)
-            nc.scalar.activation(z_bf[:, :, t], big[:], COPY, scale=gs_sb[:, t : t + 1])
+            big = keep.tile([P, S], F32, name=f"big{t}", tag=f"far{t + 1}")
+            nc.vector.tensor_tensor(big[:], st[t][:, :S], other[t][:], ALU.max)
+            nc.scalar.activation(z_pairs[:, t // 2, :, t % 2], big[:], COPY, scale=gs_sb[:, t : t + 1])
 
         def fetch_old(t, tag, align):
             old[t] = keep.tile([P, S], F32, name=f"old{t}", tag=tag, align_bytes=align)
             nc.vector.tensor_scalar(old[t][:], page[t][:].indirect(n3_list[:]), 0.5, 0.0, ALU.mult, ALU.add)
 
-        for step in range(PACK + 2):
+        for step in range(PACK + 3):
             if step < PACK:
                 subtract(step)
-            if 1 <= step <= PACK:
-                fetch(step - 1)
-            if step == PACK + 1:
+            if 2 <= step <= PACK + 1:
+                fetch(step - 2)
+            if step == PACK + 2:
                 fetch_old(0, "st1", None)
-            if step >= 2:
-                larger(step - 2)
+            if step >= 3:
+                larger(step - 3)
         fetch_old(1, "st2", None)
-        fetch_old(2, "h_pos3_0", None)
+        fetch_old(2, "other2", None)
 
+        nc.scalar.copy(
+            z_bf[:].rearrange("p s t -> p (s t)").bitcast(F32).rearrange("p (s u) -> p s u", u=2),
+            z_pairs[:].rearrange("p u s e -> p (u s e)").bitcast(F32).rearrange("p (u s) -> p s u", u=2),
+        )
         z_codes = keep.tile([P, S], U32, align_bytes=64)
         z_scale = keep.tile([P, S], U8, align_bytes=64)
         nc.vector.quantize_mx(z_codes[:].bitcast(FP8X4), z_scale[:], z_bf[:].rearrange("p s t -> p (s t)"))
@@ -165,13 +170,23 @@ def tile_picked_pqchopmxpagex_none_p_kernel(
         for t in range(PACK + 1):
             if t < PACK:
                 cols = slice(t * P, (t + 1) * P)
-                acc = psum.tile([P, S], F32, name=f"s_acc{t}")
+                acc = psum.tile([P, S], F32, name=f"s_acc{t}", tag=f"bank{t}")
                 nc.tensor.matmul_mx(
                     out=acc[:], lhsT=c_codes[:, cols].bitcast(FP8X4), lhsT_scale=c_scale[:, cols],
                     rhs=z_codes[:].bitcast(FP8X4), rhs_scale=z_scale[:], start=True, stop=True,
                 )
                 nw[t] = keep.tile([P, S], F32, name=f"nw{t}")
-                nc.vector.scalar_tensor_tensor(nw[t][:], acc[:], 0.0625, old[t][:], ALU.mult, ALU.max)
+                if t == 0:
+                    nc.vector.scalar_tensor_tensor(nw[t][:], acc[:], 0.0625, old[t][:], ALU.mult, ALU.max)
+                else:
+                    s_sb = keep.tile([P, S], F32, name=f"s_sb{t}")
+                    nc.scalar.activation(s_sb[:], acc[:], COPY, scale=0.0625)
+                    gap = keep.tile([P, S], F32, name=f"gap{t}", tag=f"turn{(t + 1) % 2}")
+                    nc.gpsimd.tensor_tensor(gap[:], old[t][:], s_sb[:], ALU.subtract)
+                    lift = keep.tile([P, S], F32, name=f"lift{t}", tag=f"turn{t % 2}")
+                    nc.scalar.activation(lift[:], gap[:], RELU)
+                    nc.gpsimd.tensor_tensor(nw[t][:], s_sb[:], lift[:], ALU.add)
             if t >= 1:
                 nc.vector.tensor_copy(page[t - 1][:].indirect(n3_list[:]), nw[t - 1][:])
-                nc.sync.dma_start(out_rows[t - 1], page[t - 1][:])
+                nc.sync.dma_start(out_rows[t - 1][:, :, : U // 2], page[t - 1][:, : U // 2])
+                (nc.scalar if t == PACK else nc.sync).dma_start(out_rows[t - 1][:, :, U // 2 :], page[t - 1][:, U // 2 :])

@@ -1,6 +1,7 @@
 from contextlib import ExitStack
 
 import concourse.mybir as mybir
+from concourse.masks import make_identity
 
 K, T, S, G, H, C, U = 512, 1024, 512, 2048, 512, 512, 1024
 FLOPS = 2 * K * H * S + 2 * K * C * S
@@ -18,7 +19,18 @@ RELU = mybir.ActivationFunctionType.Relu
 
 P = 128
 PACK = 4
+BLOCKS = K // 32
+SPREAD = P // BLOCKS
+RUN = 8
+LINE = 16
 HALF = S // 2
+ALIGN = 64
+SIXTEENTH = 0.0625
+
+FUSED_TILE = 3
+H_ORDER = (0, 1, FUSED_TILE, 2)
+Z_ORDER = (FUSED_TILE, 0, 1, 2)
+DIRECT_TILE = 0
 
 
 def tile_picked_pqchopmxpagex_none_p_kernel(
@@ -30,163 +42,188 @@ def tile_picked_pqchopmxpagex_none_p_kernel(
         psum = ctx.enter_context(tc.psum_pool(name="psum", bufs=1))
 
         def load_list(src, name):
-            t = keep.tile([P, S // 16], U16, name=name)
-            nc.sync.dma_start(t[:], src)
-            return t
+            offsets = keep.tile([P, S // 16], U16, name=name)
+            nc.sync.dma_start(offsets[:], src)
+            return offsets
 
-        def halves(lst, h):
-            return lst[:, h * (HALF // 16) : (h + 1) * (HALF // 16)]
+        def load_byte_table(table, scales, width):
+            rows = scales[0].bitcast(I32).unsqueeze(1).to_broadcast([BLOCKS, SPREAD, width // 4])
+            nc.sync.dma_start(table[:].bitcast(I32), rows)
 
-        def deal(dst, src, run):
+        def deal(dst, src, stretch):
             nc.vector.tensor_copy(
-                dst.rearrange("p (t c i) -> p c t i", t=PACK, i=run),
-                src.rearrange("p (c i t) -> p c t i", t=PACK, i=run),
+                dst.rearrange("p (t c i) -> p c t i", t=PACK, i=stretch),
+                src.rearrange("p (c i t) -> p c t i", t=PACK, i=stretch),
             )
 
-        d_byte_table = keep.tile([P, G], U8, align_bytes=64)
-        x_byte_table = keep.tile([P, T], U8, align_bytes=64)
-        planes = keep.tile([P, 2 * S], U8, align_bytes=64)
-        c_scale = keep.tile([P, C], U8, align_bytes=64)
-        nc.vector.memset(c_scale[:].bitcast(I32), 0)
-        nc.vector.memset(planes[:].bitcast(I32), 0)
+        def place(plane, picked, queues):
+            for a in range(4):
+                queues[a % 2].dma_start(plane.bitcast(I32)[a:P:32, :], picked.bitcast(I32)[SPREAD * a : P : 32, :])
+
+        d_byte_table = keep.tile([P, G], U8, align_bytes=ALIGN)
+        x_byte_table = keep.tile([P, T], U8, align_bytes=ALIGN)
+        h_scales = keep.tile([P, H + S], U8, align_bytes=ALIGN)
+        c_scale = keep.tile([P, C], U8, align_bytes=ALIGN)
+        nc.gpsimd.memset(c_scale[:].bitcast(I32), 0)
+        nc.gpsimd.memset(h_scales[:].bitcast(I32), 0)
 
         offs_list = load_list(offs, "offs_list")
-        nc.sync.dma_start(x_byte_table[:].bitcast(I32), x_scales[0].bitcast(I32).unsqueeze(1).to_broadcast([16, 8, T // 4]))
+        load_byte_table(x_byte_table, x_scales, T)
         k1_list = load_list(k1, "k1_list")
-        nc.sync.dma_start(d_byte_table[:].bitcast(I32), d_scales[0].bitcast(I32).unsqueeze(1).to_broadcast([16, 8, G // 4]))
+        load_byte_table(d_byte_table, d_scales, G)
         n2_list = load_list(n2, "n2_list")
-        d_word_table = keep.tile([P, G], I32, align_bytes=64, tag="slot0")
+        d_word_table = keep.tile([P, G], I32, align_bytes=ALIGN, tag="then_page0")
         nc.sync.dma_start(d_word_table[:], d_words[0].rearrange("p n t -> p (n t)").bitcast(I32))
-        x_word_table = keep.tile([P, T], I32, align_bytes=64, tag="slot1")
+        x_word_table = keep.tile([P, T], I32, align_bytes=ALIGN, tag="then_page1")
         nc.sync.dma_start(x_word_table[:], x_words[0].rearrange("p n t -> p (n t)").bitcast(I32))
         n3_list = load_list(n3, "n3_list")
         cand_list = load_list(cand, "cand_list")
         n1_list = load_list(n1, "n1_list")
-        h_sb = [keep.tile([P, 2 * S], F32, name=f"h{t}") for t in range(PACK)]
-        st = [keep.tile([P, 2 * S], F32, name=f"st{t}", tag=f"st{t}") for t in range(PACK)]
+
+        h_window = [keep.tile([P, 2 * S], F32, name=f"h{t}", tag=f"h{t}", align_bytes=ALIGN) for t in range(PACK)]
+        st_window = [keep.tile([P, 2 * S], F32, name=f"st{t}", tag=f"st{t}", align_bytes=ALIGN) for t in range(PACK)]
+        identity = keep.tile([P, P], F32)
+        make_identity(nc, identity[:])
         for t in range(PACK):
-            nc.vector.memset(h_sb[t][:, S:], 0.0)
-            nc.gpsimd.memset(st[t][:, S:], 0.0)
+            nc.vector.memset(h_window[t][:, S:], 0.0)
 
-        def place(plane, staged, queues):
-            src = staged.bitcast(I32)
-            dst = plane.bitcast(I32)
-            for a in range(4):
-                queues[a % 2].dma_start(dst[a:P:32, :], src[8 * a : P : 32, :])
-
-        xq_bytes = keep.tile([P, S], U8, align_bytes=64, tag="slot5")
-        d_bytes = keep.tile([P, H], U8, align_bytes=64)
-        staged = keep.tile([P, 2 * S], U8, align_bytes=64, tag="slot2")
+        xq_bytes = keep.tile([P, S], U8, align_bytes=ALIGN)
+        d_bytes = keep.tile([P, H], U8, align_bytes=ALIGN, tag="then_gs")
+        h_bytes = keep.tile([P, H + S], U8, align_bytes=ALIGN, tag="then_page2")
         nc.vector.tensor_copy(xq_bytes[:], x_byte_table[:].indirect(offs_list[:]))
         nc.vector.tensor_copy(d_bytes[:], d_byte_table[:].indirect(k1_list[:]))
-        nc.vector.tensor_copy(staged[:, S:].bitcast(I32), xq_bytes[:].bitcast(I32))
-        deal(staged[:, :S], d_bytes[:], 16)
-        place(planes[:], staged[:], (nc.sync, nc.scalar))
-        d_scale, xq_scale = planes[:, :S], planes[:, S:]
+        nc.vector.tensor_copy(h_bytes[:, H:].bitcast(I32), xq_bytes[:].bitcast(I32))
+        deal(h_bytes[:, :H], d_bytes[:], LINE)
+        place(h_scales[:], h_bytes[:], (nc.sync, nc.scalar))
+        d_scale, xq_scale = h_scales[:, :H], h_scales[:, H:]
 
-        gs_sb = keep.tile([P, PACK], F32, align_bytes=64, tag="slot5")
+        gs_sb = keep.tile([P, PACK], F32, align_bytes=ALIGN, tag="then_gs")
         nc.sync.dma_start(gs_sb[:], gs.rearrange("(p t) o -> p (t o)", t=PACK))
-        d_picked = keep.tile([P, H], U32, align_bytes=64, tag="slot3")
-        nc.vector.tensor_copy(d_picked[:], d_word_table[:].bitcast(U32).indirect(k1_list[:]))
-        xq_codes = keep.tile([P, S], U32, align_bytes=64)
-        nc.vector.tensor_copy(xq_codes[:], x_word_table[:].bitcast(U32).indirect(offs_list[:]))
-        d_codes = keep.tile([P, H], U32, align_bytes=64)
-        deal(d_codes[:].bitcast(I32), d_picked[:].bitcast(I32), 4)
 
-        for t in range(PACK):
+        d_picked = keep.tile([P, H], U32, align_bytes=ALIGN, tag="then_c_bytes")
+        nc.vector.tensor_copy(d_picked[:], d_word_table[:].bitcast(U32).indirect(k1_list[:]))
+        xq_codes = keep.tile([P, S], U32, align_bytes=ALIGN)
+        nc.vector.tensor_copy(xq_codes[:], x_word_table[:].bitcast(U32).indirect(offs_list[:]))
+        d_codes = keep.tile([P, H], U32, align_bytes=ALIGN)
+        deal(d_codes[:].bitcast(I32), d_picked[:].bitcast(I32), LINE // 4)
+
+        for t in H_ORDER:
             cols = slice(t * P, (t + 1) * P)
-            acc = psum.tile([P, S], F32, name=f"h_acc{t}", tag=f"bank{PACK + t}")
+            h_acc = psum.tile([P, S], F32, name=f"h_acc{t}", tag=f"product{t}")
             nc.tensor.matmul_mx(
-                out=acc[:], lhsT=d_codes[:, cols].bitcast(FP8X4), lhsT_scale=d_scale[:, cols],
+                out=h_acc[:], lhsT=d_codes[:, cols].bitcast(FP8X4), lhsT_scale=d_scale[:, cols],
                 rhs=xq_codes[:].bitcast(FP8X4), rhs_scale=xq_scale, start=True, stop=True,
             )
-            nc.scalar.activation(h_sb[t][:, :S], acc[:], COPY, scale=0.0625)
+            nc.scalar.activation(h_window[t][:, :S], h_acc[:], COPY, scale=-SIXTEENTH if t == FUSED_TILE else SIXTEENTH)
+            if t == FUSED_TILE:
+                nc.scalar.activation(st_window[t][:, S:], h_acc[:], COPY, scale=SIXTEENTH)
 
-        c_bytes = keep.tile([P, C], U8, align_bytes=64, tag="slot3")
+        c_bytes = keep.tile([P, C], U8, align_bytes=ALIGN, tag="then_c_bytes")
         nc.vector.tensor_copy(c_bytes[:], x_byte_table[:].indirect(cand_list[:]))
-        c_codes = keep.tile([P, C], U32, align_bytes=64)
+        c_codes = keep.tile([P, C], U32, align_bytes=ALIGN)
         nc.vector.tensor_copy(
-            c_codes[:].rearrange("p (t g v) -> p g t v", t=PACK, v=8), x_word_table[:].bitcast(U32).indirect(cand_list[:])
+            c_codes[:].rearrange("p (t g v) -> p g t v", t=PACK, v=RUN),
+            x_word_table[:].bitcast(U32).indirect(cand_list[:]),
         )
-        c_staged = keep.tile([P, C], U8, align_bytes=64, tag="slot4")
+        c_bytes_dealt = keep.tile([P, C], U8, align_bytes=ALIGN, tag="then_page3")
         nc.vector.tensor_copy(
-            c_staged[:].bitcast(I32).rearrange("p (t g w) -> p g t w", t=PACK, w=2),
-            c_bytes[:].bitcast(I32).rearrange("p (g t w) -> p g t w", t=PACK, w=2),
+            c_bytes_dealt[:].bitcast(I32).rearrange("p (t g w) -> p g t w", t=PACK, w=RUN // 4),
+            c_bytes[:].bitcast(I32).rearrange("p (g t w) -> p g t w", t=PACK, w=RUN // 4),
         )
-        place(c_scale[:], c_staged[:], (nc.sync, nc.sync))
+        place(c_scale[:], c_bytes_dealt[:], (nc.sync, nc.sync))
 
-        mem_rows = mem.rearrange("(g t v) u -> t g v u", t=PACK, v=8)
-        out_rows = out.rearrange("(g t v) u -> t g v u", t=PACK, v=8)
+        mem_rows = mem.rearrange("(g t v) u -> t g v u", t=PACK, v=RUN)
+        out_rows = out.rearrange("(g t v) u -> t g v u", t=PACK, v=RUN)
         page = []
         for t in range(PACK):
-            pg = keep.tile([P, U], F32, name=f"page{t}", tag=f"slot{(0, 1, 2, 4)[t]}", align_bytes=64)
-            nc.sync.dma_start(pg[:], mem_rows[t])
-            page.append(pg)
+            page.append(keep.tile([P, U], F32, name=f"page{t}", tag=f"then_page{t}", align_bytes=ALIGN))
+            nc.sync.dma_start(page[t][:], mem_rows[t])
 
-        z_pairs = keep.tile([P, 2, S, 2], BF16, align_bytes=64)
-        z_bf = keep.tile([P, S, PACK], BF16, align_bytes=64, tag="z_bf")
-        other, old = {}, {}
+        def add_on_tensor(a, b, name, turn):
+            turned = psum.tile([P, S], F32, name=f"{name}_turned", tag=f"turned{turn % 2}")
+            for j in range(S // P):
+                cols = slice(j * P, (j + 1) * P)
+                nc.tensor.matmul(turned[:, cols], a[:, cols], identity[:], is_transpose=True, start=True, stop=False)
+                nc.tensor.matmul(turned[:, cols], b[:, cols], identity[:], is_transpose=True, start=False, stop=True)
+            total = psum.tile([P, S], F32, name=f"{name}_total", tag=f"total{turn % 2}")
+            for half in range(2):
+                staged = keep.tile([P, HALF], F32, name=f"{name}_staged{half}", tag=f"{name}_staged{half}", align_bytes=ALIGN)
+                nc.scalar.copy(staged[:], turned[:, half * HALF : (half + 1) * HALF])
+                for j in range(HALF // P):
+                    at = half * HALF + j * P
+                    nc.tensor.transpose(total[:, at : at + P], staged[:, j * P : (j + 1) * P], identity[:])
+            return total
 
-        def subtract(t):
-            far = keep.tile([P, S], F32, name=f"far{t}", tag=f"far{t}")
-            nc.vector.tensor_copy(far[:], h_sb[t][:].indirect(n1_list[:]))
-            nc.gpsimd.tensor_tensor(st[t][:, :S], h_sb[t][:, :S], far[:], ALU.subtract)
+        for t in H_ORDER:
+            looked_up = h_window[t][:].indirect(n1_list[:])
+            if t == FUSED_TILE:
+                nc.vector.tensor_tensor(st_window[t][:, :S], looked_up, st_window[t][:, S:], ALU.add)
+            else:
+                nc.vector.tensor_scalar(st_window[t][:, S:], looked_up, -1.0, 0.0, ALU.mult, ALU.add)
+                total = add_on_tensor(h_window[t][:, :S], st_window[t][:, S:], f"st{t}", t)
+                nc.scalar.copy(st_window[t][:, :S], total[:])
 
-        def fetch(t):
-            other[t] = keep.tile([P, S], F32, name=f"other{t}", tag=f"other{t}")
-            nc.vector.tensor_copy(other[t][:], st[t][:].indirect(n2_list[:]))
-
-        def larger(t):
-            big = keep.tile([P, S], F32, name=f"big{t}", tag=f"far{t + 1}")
-            nc.vector.tensor_tensor(big[:], st[t][:, :S], other[t][:], ALU.max)
-            nc.scalar.activation(z_pairs[:, t // 2, :, t % 2], big[:], COPY, scale=gs_sb[:, t : t + 1])
-
-        def fetch_old(t, tag, align):
-            old[t] = keep.tile([P, S], F32, name=f"old{t}", tag=tag, align_bytes=align)
-            nc.vector.tensor_scalar(old[t][:], page[t][:].indirect(n3_list[:]), 0.5, 0.0, ALU.mult, ALU.add)
-
-        for step in range(PACK + 3):
+        last = Z_ORDER[-1]
+        z_pairs = keep.tile([P, 2, S, 2], BF16, align_bytes=ALIGN, tag=f"st{last}_staged0")
+        larger_tags = (f"h{last}", f"st{last}_staged1")
+        other = {}
+        for step in range(PACK + 1):
             if step < PACK:
-                subtract(step)
-            if 2 <= step <= PACK + 1:
-                fetch(step - 2)
-            if step == PACK + 2:
-                fetch_old(0, "st1", None)
-            if step >= 3:
-                larger(step - 3)
-        fetch_old(1, "st2", None)
-        fetch_old(2, "other2", None)
+                t = Z_ORDER[step]
+                other[t] = keep.tile([P, S], F32, name=f"other{t}", tag="h1" if t == FUSED_TILE else f"other{t}", align_bytes=ALIGN)
+                nc.vector.tensor_copy(other[t][:], st_window[t][:].indirect(n2_list[:]))
+            if step >= 1:
+                t = Z_ORDER[step - 1]
+                larger = keep.tile([P, S], F32, name=f"larger{t}", tag=larger_tags[(step - 1) % 2], align_bytes=ALIGN)
+                nc.vector.tensor_tensor(larger[:], st_window[t][:, :S], other[t][:], ALU.max)
+                nc.scalar.activation(z_pairs[:, t // 2, :, t % 2], larger[:], COPY, scale=gs_sb[:, t : t + 1])
 
+        old = {}
+
+        def fetch_old(t, tag):
+            old[t] = keep.tile([P, S], F32, name=f"old{t}", tag=tag, align_bytes=ALIGN)
+            factor = 0.5 if t == DIRECT_TILE else -0.5
+            nc.vector.tensor_scalar(old[t][:], page[t][:].indirect(n3_list[:]), factor, 0.0, ALU.mult, ALU.add)
+
+        fetch_old(0, f"st{last}")
+        fetch_old(1, f"other{last}")
+        z_bf = keep.tile([P, S, PACK], BF16, align_bytes=ALIGN, tag="z_bf")
         nc.scalar.copy(
             z_bf[:].rearrange("p s t -> p (s t)").bitcast(F32).rearrange("p (s u) -> p s u", u=2),
             z_pairs[:].rearrange("p u s e -> p (u s e)").bitcast(F32).rearrange("p (u s) -> p s u", u=2),
         )
-        z_codes = keep.tile([P, S], U32, align_bytes=64)
-        z_scale = keep.tile([P, S], U8, align_bytes=64)
+        z_codes = keep.tile([P, S], U32, align_bytes=ALIGN)
+        z_scale = keep.tile([P, S], U8, align_bytes=ALIGN)
         nc.vector.quantize_mx(z_codes[:].bitcast(FP8X4), z_scale[:], z_bf[:].rearrange("p s t -> p (s t)"))
-        fetch_old(3, "z_bf", 64)
+        fetch_old(2, f"st{last}_staged0")
+        fetch_old(3, "z_bf")
 
-        nw = {}
-        for t in range(PACK + 1):
-            if t < PACK:
-                cols = slice(t * P, (t + 1) * P)
-                acc = psum.tile([P, S], F32, name=f"s_acc{t}", tag=f"bank{t}")
-                nc.tensor.matmul_mx(
-                    out=acc[:], lhsT=c_codes[:, cols].bitcast(FP8X4), lhsT_scale=c_scale[:, cols],
-                    rhs=z_codes[:].bitcast(FP8X4), rhs_scale=z_scale[:], start=True, stop=True,
-                )
-                nw[t] = keep.tile([P, S], F32, name=f"nw{t}")
-                if t == 0:
-                    nc.vector.scalar_tensor_tensor(nw[t][:], acc[:], 0.0625, old[t][:], ALU.mult, ALU.max)
-                else:
-                    s_sb = keep.tile([P, S], F32, name=f"s_sb{t}")
-                    nc.scalar.activation(s_sb[:], acc[:], COPY, scale=0.0625)
-                    gap = keep.tile([P, S], F32, name=f"gap{t}", tag=f"turn{(t + 1) % 2}")
-                    nc.gpsimd.tensor_tensor(gap[:], old[t][:], s_sb[:], ALU.subtract)
-                    lift = keep.tile([P, S], F32, name=f"lift{t}", tag=f"turn{t % 2}")
-                    nc.scalar.activation(lift[:], gap[:], RELU)
-                    nc.gpsimd.tensor_tensor(nw[t][:], s_sb[:], lift[:], ALU.add)
-            if t >= 1:
-                nc.vector.tensor_copy(page[t - 1][:].indirect(n3_list[:]), nw[t - 1][:])
-                nc.sync.dma_start(out_rows[t - 1][:, :, : U // 2], page[t - 1][:, : U // 2])
-                (nc.scalar if t == PACK else nc.sync).dma_start(out_rows[t - 1][:, :, U // 2 :], page[t - 1][:, U // 2 :])
+        def score(t):
+            cols = slice(t * P, (t + 1) * P)
+            s_acc = psum.tile([P, S], F32, name=f"s_acc{t}", tag="product0" if t == DIRECT_TILE else "product1")
+            nc.tensor.matmul_mx(
+                out=s_acc[:], lhsT=c_codes[:, cols].bitcast(FP8X4), lhsT_scale=c_scale[:, cols],
+                rhs=z_codes[:].bitcast(FP8X4), rhs_scale=z_scale[:], start=True, stop=True,
+            )
+            return s_acc
+
+        def store(t):
+            nc.sync.dma_start(out_rows[t][:, :, : U // 2], page[t][:, : U // 2])
+            (nc.scalar if t == PACK - 1 else nc.sync).dma_start(out_rows[t][:, :, U // 2 :], page[t][:, U // 2 :])
+
+        s_next = score(DIRECT_TILE + 1)
+        new_direct = keep.tile([P, S], F32)
+        nc.vector.scalar_tensor_tensor(new_direct[:], score(DIRECT_TILE)[:], SIXTEENTH, old[DIRECT_TILE][:], ALU.mult, ALU.max)
+        nc.vector.tensor_copy(page[DIRECT_TILE][:].indirect(n3_list[:]), new_direct[:])
+        store(DIRECT_TILE)
+
+        for t in range(DIRECT_TILE + 1, PACK):
+            s_sb = keep.tile([P, S], F32, name=f"s_sb{t}")
+            nc.scalar.activation(s_sb[:], s_next[:], COPY, scale=SIXTEENTH)
+            lead = add_on_tensor(s_sb[:], old[t][:], f"lead{t}", t)
+            if t + 1 < PACK:
+                s_next = score(t + 1)
+            lift = keep.tile([P, S], F32, name=f"lift{t}")
+            nc.scalar.activation(lift[:], lead[:], RELU, scale=-1.0)
+            nc.vector.tensor_tensor(page[t][:].indirect(n3_list[:]), s_sb[:], lift[:], ALU.add)
+            store(t)

from contextlib import ExitStack

import concourse.mybir as mybir
from concourse.masks import make_identity

K, T, S, G, H, C, U = 512, 1024, 512, 2048, 512, 512, 1024
FLOPS = 2 * K * H * S + 2 * K * C * S

F32 = mybir.dt.float32
BF16 = mybir.dt.bfloat16
I32 = mybir.dt.int32
U32 = mybir.dt.uint32
U16 = mybir.dt.uint16
U8 = mybir.dt.uint8
FP8X4 = mybir.dt.float8_e4m3fn_x4
ALU = mybir.AluOpType
COPY = mybir.ActivationFunctionType.Copy
RELU = mybir.ActivationFunctionType.Relu

P = 128
PACK = 4
BLOCKS = K // 32
SPREAD = P // BLOCKS
RUN = 8
LINE = 16
HALF = S // 2
ALIGN = 64
SIXTEENTH = 0.0625

FUSED_TILE = 3
H_ORDER = (0, 1, FUSED_TILE, 2)
Z_ORDER = (FUSED_TILE, 0, 1, 2)
DIRECT_TILE = 0


def tile_picked_pqchopmxpagex_none_p_kernel(
    tc, x_words, x_scales, d_words, d_scales, gs, mem, offs, k1, n1, n2, cand, n3, out
):
    nc = tc.nc
    with ExitStack() as ctx:
        keep = ctx.enter_context(tc.tile_pool(name="keep", bufs=1))
        psum = ctx.enter_context(tc.psum_pool(name="psum", bufs=1))

        def load_list(src, name):
            offsets = keep.tile([P, S // 16], U16, name=name)
            nc.sync.dma_start(offsets[:], src)
            return offsets

        def load_byte_table(table, scales, width):
            rows = scales[0].bitcast(I32).unsqueeze(1).to_broadcast([BLOCKS, SPREAD, width // 4])
            nc.sync.dma_start(table[:].bitcast(I32), rows)

        def deal(dst, src, stretch):
            nc.vector.tensor_copy(
                dst.rearrange("p (t c i) -> p c t i", t=PACK, i=stretch),
                src.rearrange("p (c i t) -> p c t i", t=PACK, i=stretch),
            )

        def place(plane, picked, queues):
            for a in range(4):
                queues[a % 2].dma_start(plane.bitcast(I32)[a:P:32, :], picked.bitcast(I32)[SPREAD * a : P : 32, :])

        d_byte_table = keep.tile([P, G], U8, align_bytes=ALIGN)
        x_byte_table = keep.tile([P, T], U8, align_bytes=ALIGN)
        h_scales = keep.tile([P, H + S], U8, align_bytes=ALIGN)
        c_scale = keep.tile([P, C], U8, align_bytes=ALIGN)
        nc.gpsimd.memset(c_scale[:].bitcast(I32), 0)
        nc.gpsimd.memset(h_scales[:].bitcast(I32), 0)

        offs_list = load_list(offs, "offs_list")
        load_byte_table(x_byte_table, x_scales, T)
        k1_list = load_list(k1, "k1_list")
        load_byte_table(d_byte_table, d_scales, G)
        n2_list = load_list(n2, "n2_list")
        d_word_table = keep.tile([P, G], I32, align_bytes=ALIGN, tag="then_page0")
        nc.sync.dma_start(d_word_table[:], d_words[0].rearrange("p n t -> p (n t)").bitcast(I32))
        x_word_table = keep.tile([P, T], I32, align_bytes=ALIGN, tag="then_page1")
        nc.sync.dma_start(x_word_table[:], x_words[0].rearrange("p n t -> p (n t)").bitcast(I32))
        n3_list = load_list(n3, "n3_list")
        cand_list = load_list(cand, "cand_list")
        n1_list = load_list(n1, "n1_list")

        h_window = [keep.tile([P, 2 * S], F32, name=f"h{t}", tag=f"h{t}", align_bytes=ALIGN) for t in range(PACK)]
        st_window = [keep.tile([P, 2 * S], F32, name=f"st{t}", tag=f"st{t}", align_bytes=ALIGN) for t in range(PACK)]
        identity = keep.tile([P, P], F32)
        make_identity(nc, identity[:])
        for t in range(PACK):
            nc.vector.memset(h_window[t][:, S:], 0.0)

        xq_bytes = keep.tile([P, S], U8, align_bytes=ALIGN)
        d_bytes = keep.tile([P, H], U8, align_bytes=ALIGN, tag="then_gs")
        h_bytes = keep.tile([P, H + S], U8, align_bytes=ALIGN, tag="then_page2")
        nc.vector.tensor_copy(xq_bytes[:], x_byte_table[:].indirect(offs_list[:]))
        nc.vector.tensor_copy(d_bytes[:], d_byte_table[:].indirect(k1_list[:]))
        nc.vector.tensor_copy(h_bytes[:, H:].bitcast(I32), xq_bytes[:].bitcast(I32))
        deal(h_bytes[:, :H], d_bytes[:], LINE)
        place(h_scales[:], h_bytes[:], (nc.sync, nc.scalar))
        d_scale, xq_scale = h_scales[:, :H], h_scales[:, H:]

        gs_sb = keep.tile([P, PACK], F32, align_bytes=ALIGN, tag="then_gs")
        nc.sync.dma_start(gs_sb[:], gs.rearrange("(p t) o -> p (t o)", t=PACK))

        d_picked = keep.tile([P, H], U32, align_bytes=ALIGN, tag="then_c_bytes")
        nc.vector.tensor_copy(d_picked[:], d_word_table[:].bitcast(U32).indirect(k1_list[:]))
        xq_codes = keep.tile([P, S], U32, align_bytes=ALIGN)
        nc.vector.tensor_copy(xq_codes[:], x_word_table[:].bitcast(U32).indirect(offs_list[:]))
        d_codes = keep.tile([P, H], U32, align_bytes=ALIGN)
        deal(d_codes[:].bitcast(I32), d_picked[:].bitcast(I32), LINE // 4)

        for t in H_ORDER:
            cols = slice(t * P, (t + 1) * P)
            h_acc = psum.tile([P, S], F32, name=f"h_acc{t}", tag=f"product{t}")
            nc.tensor.matmul_mx(
                out=h_acc[:], lhsT=d_codes[:, cols].bitcast(FP8X4), lhsT_scale=d_scale[:, cols],
                rhs=xq_codes[:].bitcast(FP8X4), rhs_scale=xq_scale, start=True, stop=True,
            )
            nc.scalar.activation(h_window[t][:, :S], h_acc[:], COPY, scale=-SIXTEENTH if t == FUSED_TILE else SIXTEENTH)
            if t == FUSED_TILE:
                nc.scalar.activation(st_window[t][:, S:], h_acc[:], COPY, scale=SIXTEENTH)

        c_bytes = keep.tile([P, C], U8, align_bytes=ALIGN, tag="then_c_bytes")
        nc.vector.tensor_copy(c_bytes[:], x_byte_table[:].indirect(cand_list[:]))
        c_codes = keep.tile([P, C], U32, align_bytes=ALIGN)
        nc.vector.tensor_copy(
            c_codes[:].rearrange("p (t g v) -> p g t v", t=PACK, v=RUN),
            x_word_table[:].bitcast(U32).indirect(cand_list[:]),
        )
        c_bytes_dealt = keep.tile([P, C], U8, align_bytes=ALIGN, tag="then_page3")
        nc.vector.tensor_copy(
            c_bytes_dealt[:].bitcast(I32).rearrange("p (t g w) -> p g t w", t=PACK, w=RUN // 4),
            c_bytes[:].bitcast(I32).rearrange("p (g t w) -> p g t w", t=PACK, w=RUN // 4),
        )
        place(c_scale[:], c_bytes_dealt[:], (nc.sync, nc.sync))

        mem_rows = mem.rearrange("(g t v) u -> t g v u", t=PACK, v=RUN)
        out_rows = out.rearrange("(g t v) u -> t g v u", t=PACK, v=RUN)
        page = []
        for t in range(PACK):
            page.append(keep.tile([P, U], F32, name=f"page{t}", tag=f"then_page{t}", align_bytes=ALIGN))
            nc.sync.dma_start(page[t][:], mem_rows[t])

        def add_on_tensor(a, b, name, turn):
            turned = psum.tile([P, S], F32, name=f"{name}_turned", tag=f"turned{turn % 2}")
            for j in range(S // P):
                cols = slice(j * P, (j + 1) * P)
                nc.tensor.matmul(turned[:, cols], a[:, cols], identity[:], is_transpose=True, start=True, stop=False)
                nc.tensor.matmul(turned[:, cols], b[:, cols], identity[:], is_transpose=True, start=False, stop=True)
            total = psum.tile([P, S], F32, name=f"{name}_total", tag=f"total{turn % 2}")
            for half in range(2):
                staged = keep.tile([P, HALF], F32, name=f"{name}_staged{half}", tag=f"{name}_staged{half}", align_bytes=ALIGN)
                nc.scalar.copy(staged[:], turned[:, half * HALF : (half + 1) * HALF])
                for j in range(HALF // P):
                    at = half * HALF + j * P
                    nc.tensor.transpose(total[:, at : at + P], staged[:, j * P : (j + 1) * P], identity[:])
            return total

        for t in H_ORDER:
            looked_up = h_window[t][:].indirect(n1_list[:])
            if t == FUSED_TILE:
                nc.vector.tensor_tensor(st_window[t][:, :S], looked_up, st_window[t][:, S:], ALU.add)
            else:
                nc.vector.tensor_scalar(st_window[t][:, S:], looked_up, -1.0, 0.0, ALU.mult, ALU.add)
                total = add_on_tensor(h_window[t][:, :S], st_window[t][:, S:], f"st{t}", t)
                nc.scalar.copy(st_window[t][:, :S], total[:])

        last = Z_ORDER[-1]
        z_pairs = keep.tile([P, 2, S, 2], BF16, align_bytes=ALIGN, tag=f"st{last}_staged0")
        larger_tags = (f"h{last}", f"st{last}_staged1")
        other = {}
        for step in range(PACK + 1):
            if step < PACK:
                t = Z_ORDER[step]
                other[t] = keep.tile([P, S], F32, name=f"other{t}", tag="h1" if t == FUSED_TILE else f"other{t}", align_bytes=ALIGN)
                nc.vector.tensor_copy(other[t][:], st_window[t][:].indirect(n2_list[:]))
            if step >= 1:
                t = Z_ORDER[step - 1]
                larger = keep.tile([P, S], F32, name=f"larger{t}", tag=larger_tags[(step - 1) % 2], align_bytes=ALIGN)
                nc.vector.tensor_tensor(larger[:], st_window[t][:, :S], other[t][:], ALU.max)
                nc.scalar.activation(z_pairs[:, t // 2, :, t % 2], larger[:], COPY, scale=gs_sb[:, t : t + 1])

        old = {}

        def fetch_old(t, tag):
            old[t] = keep.tile([P, S], F32, name=f"old{t}", tag=tag, align_bytes=ALIGN)
            factor = 0.5 if t == DIRECT_TILE else -0.5
            nc.vector.tensor_scalar(old[t][:], page[t][:].indirect(n3_list[:]), factor, 0.0, ALU.mult, ALU.add)

        fetch_old(0, f"st{last}")
        fetch_old(1, f"other{last}")
        z_bf = keep.tile([P, S, PACK], BF16, align_bytes=ALIGN, tag="z_bf")
        nc.scalar.copy(
            z_bf[:].rearrange("p s t -> p (s t)").bitcast(F32).rearrange("p (s u) -> p s u", u=2),
            z_pairs[:].rearrange("p u s e -> p (u s e)").bitcast(F32).rearrange("p (u s) -> p s u", u=2),
        )
        z_codes = keep.tile([P, S], U32, align_bytes=ALIGN)
        z_scale = keep.tile([P, S], U8, align_bytes=ALIGN)
        nc.vector.quantize_mx(z_codes[:].bitcast(FP8X4), z_scale[:], z_bf[:].rearrange("p s t -> p (s t)"))
        fetch_old(2, f"st{last}_staged0")
        fetch_old(3, "z_bf")

        def score(t):
            cols = slice(t * P, (t + 1) * P)
            s_acc = psum.tile([P, S], F32, name=f"s_acc{t}", tag="product0" if t == DIRECT_TILE else "product1")
            nc.tensor.matmul_mx(
                out=s_acc[:], lhsT=c_codes[:, cols].bitcast(FP8X4), lhsT_scale=c_scale[:, cols],
                rhs=z_codes[:].bitcast(FP8X4), rhs_scale=z_scale[:], start=True, stop=True,
            )
            return s_acc

        def store(t):
            nc.sync.dma_start(out_rows[t][:, :, : U // 2], page[t][:, : U // 2])
            (nc.scalar if t == PACK - 1 else nc.sync).dma_start(out_rows[t][:, :, U // 2 :], page[t][:, U // 2 :])

        s_next = score(DIRECT_TILE + 1)
        new_direct = keep.tile([P, S], F32)
        nc.vector.scalar_tensor_tensor(new_direct[:], score(DIRECT_TILE)[:], SIXTEENTH, old[DIRECT_TILE][:], ALU.mult, ALU.max)
        nc.vector.tensor_copy(page[DIRECT_TILE][:].indirect(n3_list[:]), new_direct[:])
        store(DIRECT_TILE)

        for t in range(DIRECT_TILE + 1, PACK):
            s_sb = keep.tile([P, S], F32, name=f"s_sb{t}")
            nc.scalar.activation(s_sb[:], s_next[:], COPY, scale=SIXTEENTH)
            lead = add_on_tensor(s_sb[:], old[t][:], f"lead{t}", t)
            if t + 1 < PACK:
                s_next = score(t + 1)
            lift = keep.tile([P, S], F32, name=f"lift{t}")
            nc.scalar.activation(lift[:], lead[:], RELU, scale=-1.0)
            nc.vector.tensor_tensor(page[t][:].indirect(n3_list[:]), s_sb[:], lift[:], ALU.add)
            store(t)
